import numpy as np
import ml_dtypes


def mxq(x, axis, fmt="e4m3"):
    dtype, down = {"e4m3": (ml_dtypes.float8_e4m3fn, 7), "e5m2": (ml_dtypes.float8_e5m2, 14)}[fmt]
    v = np.moveaxis(np.asarray(x, np.float32).astype(ml_dtypes.bfloat16).astype(np.float64), axis, -1)
    blocks = v.reshape(v.shape[:-1] + (-1, 32))
    amax = np.abs(blocks).max(-1, keepdims=True)
    byte = np.maximum(np.where(amax > 0, np.frexp(amax)[1] - 1 + 127, 0) - down, 1)
    scale = np.exp2(byte - 127.0)
    codes = (blocks / scale).astype(np.float32).astype(dtype).astype(np.float64)
    return np.moveaxis((codes * scale).reshape(v.shape), -1, axis)


WIDE = False


def mx_kscale(k):
    if not WIDE:
        return np.ones(k)
    levels = np.array([10, -10, 5, -5, 0])
    if k % 512:
        return np.exp2(np.random.permutation(np.resize(levels, k // 32))).repeat(32)
    a = np.empty((k // 512, 16))
    for p in range(k // 512):
        a[p, :8] = np.random.permutation(np.resize(levels, 8))
        for g in range(8):
            far = levels[np.abs(levels - a[p, g]) >= 10]
            a[p, g + 8] = far[np.random.randint(len(far))]
    return np.exp2(a.ravel()).repeat(32)


def f64(x):
    return np.asarray(x).astype(np.float64)


def striped(idx):
    return np.tile(idx.reshape(-1, 16).T, (8, 1)).astype(np.uint16)


def unstriped(offs):
    return offs[:16].T.reshape(-1).astype(np.int64)


def striped8(idx):
    return np.concatenate([x.reshape(-1, 16).T for x in idx]).astype(np.uint16)


def runs(offs, k):
    lists = np.stack([offs[16 * r : 16 * r + 16].T.reshape(-1) for r in range(8)]).astype(np.int64)
    return lists[np.arange(k) % 512 // 64]


def pack_weight(w):
    k, n = w.shape
    w = f64(np.asarray(w, np.float32).astype(ml_dtypes.bfloat16)).reshape(k // 32, 32, n)
    amax = np.abs(w).max(1)
    byte = np.clip(np.where(amax > 0, np.frexp(amax)[1] - 1 + 127 - 7, 1), 1, 254)
    scaled = (w * np.exp2(127.0 - byte)[:, None, :]).reshape(k, n).astype(np.float32)
    words = np.ascontiguousarray(scaled.reshape(k // 512, 128, 4, n).transpose(0, 1, 3, 2)).astype(ml_dtypes.float8_e4m3fn).view(np.uint8)
    return words, np.ascontiguousarray(byte.astype(np.uint8).reshape(k // 512, 16, n))


def unpack_weight(words, scales):
    g, p, n, _ = words.shape
    vals = np.ascontiguousarray(words).view(ml_dtypes.float8_e4m3fn).astype(np.float64) * np.repeat(np.exp2(scales.astype(np.float64) - 127.0), 8, axis=1)[..., None]
    return vals.transpose(0, 1, 3, 2).reshape(g * 512, n)


def sigmoid(v):
    return 1.0 / (1.0 + np.exp(-np.maximum(v, -700.0)))


K, T, S, V, H, W = 512, 2048, 512, 512, 512, 256


def setup_inputs():
    n = np.random.standard_normal
    s = mx_kscale(K)[:, None]
    u = mx_kscale(S)
    packed_xT = pack_weight(n((K, T)) * s)
    perm = np.stack([np.random.permutation(S) for _ in range(8)])
    return {
        "x_words": packed_xT[0],
        "x_scales": packed_xT[1],
        "w1": (n((K, H)) / np.sqrt(K) / s).astype(np.float32),
        "w2": (n((K, H)) / np.sqrt(K) / s).astype(np.float32),
        "ga": (np.random.uniform(0.5, 1.5, (H, 1)) * u[:, None]).astype(np.float32),
        "gb": (np.random.uniform(0.5, 1.5, (H, 1)) / u[:, None]).astype(np.float32),
        "offs": striped(np.random.permutation(T)[:S]),
        "two": striped(np.random.permutation(T)[:V]),
        "n1": striped8(perm[:, :W]),
        "n2": striped8(perm[:, W:]),
        "n3": striped8(np.stack([np.random.permutation(V) for _ in range(8)])),
        "n4": striped8(np.stack([np.random.permutation(V) for _ in range(8)])),
        "n5": striped8(np.stack([np.random.permutation(V) for _ in range(8)])),
        "n6": striped8(np.stack([np.random.permutation(V) for _ in range(8)])),
        "n7": striped8(np.stack([np.random.permutation(V) for _ in range(8)])),
    }


def reference(x_words, x_scales, w1, w2, ga, gb, offs, two, n1, n2, n3, n4, n5, n6, n7):
    xq = unpack_weight(x_words, x_scales)[:, unstriped(offs)]
    a = mxq(f64(w1), 0, "e4m3").T @ xq
    pa = a[np.arange(H)[:, None], runs(n1, H)]
    pb = a[np.arange(H)[:, None], runs(n2, H)]
    rb = np.minimum(pa, pb)
    ra = np.maximum(pa, pb)
    ds = np.zeros((H, S))
    ds[np.arange(H)[:, None], runs(n1, H)] = ra
    dt = ds.copy()
    dt[np.arange(H)[:, None], runs(n2, H)] = rb
    z = f64(ga) * dt
    x_two = unpack_weight(x_words, x_scales)[:, unstriped(two)]
    b = mxq(f64(w2), 0, "e4m3").T @ x_two
    z2 = f64(gb) * (b * (b[np.arange(H)[:, None], runs(n3, H)] - (b[np.arange(H)[:, None], runs(n4, H)])))
    s = 0.0625 * ((mxq(z, 0, "e4m3").T @ mxq(z2, 0, "e4m3")))
    return (s[np.arange(S)[:, None], runs(n5, S)]) * sigmoid(s) + (s[np.arange(S)[:, None], runs(n6, S)]) * (sigmoid(s[np.arange(S)[:, None], runs(n7, S)]))

@@ -1,0 +1,228 @@
+from contextlib import ExitStack
+
+import concourse.mybir as mybir
+
+F32 = mybir.dt.float32
+BF16 = mybir.dt.bfloat16
+U32 = mybir.dt.uint32
+I32 = mybir.dt.int32
+U16 = mybir.dt.uint16
+U8 = mybir.dt.uint8
+FP8X4 = mybir.dt.float8_e4m3fn_x4
+ALU = mybir.AluOpType
+ACT = mybir.ActivationFunctionType
+
+P = 128
+PACK = 4
+T = 2048
+N = 512
+W = 256
+FLOPS = 3 * 2 * 512 * 512 * 512
+
+
+def tile_picked_kqorderwindwsum_none_p_kernel(
+    tc, x_words, x_scales, w1, w2, ga, gb, offs, two, n1, n2, n3, n4, n5, n6, n7, out
+):
+    nc = tc.nc
+    with ExitStack() as ctx:
+        keep = ctx.enter_context(tc.tile_pool(name="keep", bufs=1))
+        psum = ctx.enter_context(tc.psum_pool(name="psum", bufs=1))
+
+        def load_list(name, src):
+            tile = keep.tile([P, src.shape[1]], U16, name=name)
+            nc.sync.dma_start(tile[:], src)
+            return tile
+
+        def load_weight(name, src):
+            raw = keep.tile([P, PACK, N], F32, name=name)
+            nc.sync.dma_start(raw[:], src.rearrange("(p j) c -> p j c", j=PACK))
+            return raw
+
+        def load_gain(name, src):
+            tile = keep.tile([P, PACK], F32, name=name)
+            nc.sync.dma_start(tile[:], src.rearrange("(p t) o -> p (t o)", t=PACK))
+            return tile
+
+        table_scales = keep.tile([P, T], U8, name="table_scales", align_bytes=64)
+        nc.vector.memset(table_scales[:].bitcast(I32), 0)
+        warm = keep.tile([P, 2], F32, name="warm")
+        nc.vector.memset(warm[:, 0:1], 0.0)
+
+        two_l = load_list("two_l", two)
+        offs_l = load_list("offs_l", offs)
+        w2_view = w2.rearrange("(p j) c -> p j c", j=PACK)
+        w2_raw = [keep.tile([P, PACK, N // 2], F32, name="w2_raw%d" % h) for h in range(2)]
+        nc.sync.dma_start(w2_raw[0][:], w2_view[:, :, : N // 2])
+        for q in range(4):
+            nc.sync.dma_start(
+                table_scales[32 * q : 32 * q + 4, :].bitcast(I32), x_scales[0, 4 * q : 4 * q + 4, :].bitcast(I32)
+            )
+        nc.sync.dma_start(w2_raw[1][:], w2_view[:, :, N // 2 :])
+        table_words = keep.tile([P, T], U32, name="table_words", align_bytes=64)
+        nc.sync.dma_start(table_words[:].bitcast(I32), x_words[0].rearrange("p n t -> p (n t)").bitcast(I32))
+        nc.scalar.activation(warm[:, 1:2], warm[:, 0:1], ACT.Sigmoid)
+        gb_t = load_gain("gb_t", gb)
+        n4_l = load_list("n4_l", n4)
+        n3_l = load_list("n3_l", n3)
+        w1_raw = load_weight("w1_raw", w1)
+        ga_t = load_gain("ga_t", ga)
+        n1_l = load_list("n1_l", n1)
+        n2_l = load_list("n2_l", n2)
+        n5_l = load_list("n5_l", n5)
+        n6_l = load_list("n6_l", n6)
+        n7_l = load_list("n7_l", n7)
+
+        def mx_tiles(name):
+            codes = keep.tile([P, N], U32, name=name + "_codes", align_bytes=64)
+            scales = keep.tile([P, N], U8, name=name + "_scales", align_bytes=64)
+            return codes, scales
+
+        xb = mx_tiles("xb")
+        xa = mx_tiles("xa")
+        nc.vector.tensor_copy(xb[1][:], table_scales[:].indirect(two_l[:]))
+        nc.vector.tensor_copy(xa[1][:], table_scales[:].indirect(offs_l[:]))
+
+        def weave_weight(name, raws):
+            woven = keep.tile([P, PACK * N], BF16, name=name, align_bytes=64)
+            dst = woven[:].rearrange("p (t m j) -> p m j t", t=PACK, j=PACK)
+            share = P // len(raws)
+            for h, raw in enumerate(raws):
+                nc.scalar.copy(dst[:, h * share : (h + 1) * share], raw[:].rearrange("p j (m t) -> p m j t", t=PACK))
+            return woven
+
+        def quantise(pair, cols, src):
+            nc.vector.quantize_mx(out=pair[0][:, cols].bitcast(FP8X4), scales=pair[1][:, cols], in_=src)
+
+        def product(acc, stationary, t, moving, span):
+            cols = slice(P * t, P * (t + 1))
+            nc.tensor.matmul_mx(
+                out=acc,
+                lhsT=stationary[0][:, cols].bitcast(FP8X4),
+                lhsT_scale=stationary[1][:, cols],
+                rhs=moving[0][:, span].bitcast(FP8X4),
+                rhs_scale=moving[1][:, span],
+                start=True,
+                stop=True,
+            )
+
+        w2_woven = weave_weight("w2_woven", w2_raw)
+        w2q = mx_tiles("w2q")
+        quantise(w2q, slice(0, N), w2_woven[:])
+        nc.vector.tensor_copy(xb[0][:], table_words[:].indirect(two_l[:]))
+        nc.vector.tensor_copy(xa[0][:], table_words[:].indirect(offs_l[:]))
+
+        wide = [keep.tile([P, 2 * N], F32, name="wide%d" % t) for t in range(PACK)]
+        b_banks = [psum.tile([P, N], F32, name="bank%d" % t) for t in range(PACK)]
+        for t in range(PACK):
+            product(b_banks[t][:], w2q, t, xb, slice(0, N))
+            nc.scalar.copy(wide[t][:, :N], b_banks[t][:])
+
+        w1_woven = weave_weight("w1_woven", [w1_raw])
+        w1q = mx_tiles("w1q")
+
+        z2_planes = keep.tile([P, PACK, N], BF16, name="z2_planes")
+        b4 = [keep.tile([P, N], F32, name="b4_%d" % t) for t in range(PACK)]
+        diff = [keep.tile([P, N], F32, name="diff%d" % t) for t in range(PACK)]
+        for step in range(PACK + 2):
+            if step < PACK:
+                nc.vector.tensor_copy(b4[step][:], wide[step][:].indirect(n4_l[:]))
+            if 1 <= step <= PACK:
+                t = step - 1
+                nc.vector.tensor_tensor(diff[t][:], wide[t][:].indirect(n3_l[:]), b4[t][:], ALU.subtract)
+            if step >= 2:
+                t = step - 2
+                nc.vector.scalar_tensor_tensor(
+                    z2_planes[:, t, :], diff[t][:], gb_t[:, t : t + 1], b_banks[t][:], ALU.mult, ALU.mult
+                )
+            if step == 3:
+                quantise(w1q, slice(0, N), w1_woven[:])
+
+        a_rows = [keep.tile([P, N], F32, name="a%d" % t) for t in range(PACK)]
+        for t in range(PACK):
+            bank = psum.tile([P, N], F32, name="bank%d" % (PACK + t))
+            product(bank[:], w1q, t, xa, slice(0, N))
+            nc.scalar.copy(a_rows[t][:], bank[:])
+
+        z2_woven = keep.tile([P, PACK * N], BF16, name="z2_woven", align_bytes=64)
+        nc.scalar.copy(
+            z2_woven[:].rearrange("p (c i t) -> p c t i", i=4, t=PACK),
+            z2_planes[:].rearrange("p t (c i) -> p c t i", i=4),
+        )
+        z2q = mx_tiles("z2q")
+
+        pa = keep.tile([P, PACK, W], F32, name="pa")
+        pb = keep.tile([P, PACK, W], F32, name="pb")
+        ra = keep.tile([P, PACK, W], F32, name="ra")
+        rb = keep.tile([P, PACK, W], F32, name="rb")
+        for t in range(PACK):
+            nc.vector.tensor_copy(pa[:, t, :], a_rows[t][:].indirect(n1_l[:]))
+            nc.vector.tensor_copy(pb[:, t, :], a_rows[t][:].indirect(n2_l[:]))
+        for h in range(2):
+            pair = slice(2 * h, 2 * h + 2)
+            nc.vector.tensor_tensor(ra[:, pair, :], pa[:, pair, :], pb[:, pair, :], ALU.max)
+            nc.vector.tensor_tensor(rb[:, pair, :], pa[:, pair, :], pb[:, pair, :], ALU.min)
+        quantise(z2q, slice(0, N), z2_woven[:])
+
+        dt_rows = [keep.tile([P, N], F32, name="dt%d" % t) for t in range(PACK)]
+        z_woven = keep.tile([P, PACK * N], BF16, name="z_woven", align_bytes=64)
+        z_slots = z_woven[:].rearrange("p (u m t) -> p t u m", u=PACK, t=PACK)
+        for h in range(2):
+            for t in (2 * h, 2 * h + 1):
+                nc.vector.tensor_copy(dt_rows[t][:].indirect(n1_l[:]), ra[:, t, :])
+            for t in (2 * h, 2 * h + 1):
+                nc.vector.tensor_copy(dt_rows[t][:].indirect(n2_l[:]), rb[:, t, :])
+                if t < PACK - 1:
+                    nc.scalar.activation(
+                        z_slots[:, t],
+                        dt_rows[t][:].rearrange("p (m u) -> p u m", u=PACK),
+                        ACT.Copy,
+                        scale=ga_t[:, t : t + 1],
+                    )
+
+        zq = mx_tiles("zq")
+        last = PACK - 1
+        for u in range(PACK):
+            nc.scalar.activation(
+                z_slots[:, last, u],
+                dt_rows[last][:].rearrange("p (m u) -> p u m", u=PACK)[:, u],
+                ACT.Copy,
+                scale=ga_t[:, last : last + 1],
+            )
+            quantise(zq, slice(P * u, P * (u + 1)), z_woven[:, N * u : N * (u + 1)])
+
+        out_rows = out.rearrange("(p u) v -> u p v", u=PACK)
+        sig = [keep.tile([P, N], F32, name="sig%d" % u) for u in range(PACK)]
+        sig7 = [keep.tile([P, N], F32, name="sig7_%d" % u) for u in range(PACK)]
+        for u in range(PACK):
+            if u == 0:
+                halves = [slice(0, N // 2), slice(N // 2, N)]
+                banks = [psum.tile([P, N], F32, name="bank%d" % (PACK * h)) for h in range(2)]
+                for h in range(2):
+                    product(banks[h][:, : N // 2], zq, u, z2q, halves[h])
+                for h in range(2):
+                    nc.scalar.activation(sig[u][:, halves[h]], banks[h][:, : N // 2], ACT.Sigmoid, scale=0.0625)
+                    nc.vector.tensor_scalar_mul(wide[u][:, halves[1 - h]], banks[1 - h][:, : N // 2], 0.0625)
+            else:
+                bank = psum.tile([P, N], F32, name="bank%d" % u)
+                product(bank[:], zq, u, z2q, slice(0, N))
+                nc.scalar.activation(wide[u][:, :N], bank[:], ACT.Copy, scale=0.0625)
+                nc.scalar.activation(sig[u][:], bank[:], ACT.Sigmoid, scale=0.0625)
+            nc.scalar.activation(sig7[u][:], wide[u][:].indirect(n7_l[:]), ACT.Sigmoid)
+
+        pieces = [(u, 0, N) for u in range(PACK - 1)] + [(PACK - 1, 0, N // 2), (PACK - 1, N // 2, N)]
+        term5 = [keep.tile([P, N], F32, name="term5_%d" % u) for u in range(PACK)]
+        term6 = [keep.tile([P, N], F32, name="term6_%d" % u) for u in range(PACK)]
+        total = [keep.tile([P, N], F32, name="total%d" % u) for u in range(PACK)]
+
+        def finish(piece):
+            u, c0, c1 = piece
+            nc.vector.tensor_tensor(total[u][:, c0:c1], term5[u][:, c0:c1], term6[u][:, c0:c1], ALU.add)
+            nc.sync.dma_start(out_rows[u][:, c0:c1], total[u][:, c0:c1])
+
+        for i, (u, c0, c1) in enumerate(pieces):
+            entries = slice(c0 // 16, c1 // 16)
+            nc.vector.tensor_tensor(term5[u][:, c0:c1], wide[u][:].indirect(n5_l[:, entries]), sig[u][:, c0:c1], ALU.mult)
+            if i >= 1:
+                finish(pieces[i - 1])
+            nc.vector.tensor_tensor(term6[u][:, c0:c1], wide[u][:].indirect(n6_l[:, entries]), sig7[u][:, c0:c1], ALU.mult)
+        finish(pieces[-1])

@@ -33,11 +33,6 @@ def tile_picked_kqorderwindwsum_none_p_kernel(
             nc.sync.dma_start(tile[:], src)
             return tile
 
-        def load_weight(name, src):
-            raw = keep.tile([P, PACK, N], F32, name=name)
-            nc.sync.dma_start(raw[:], src.rearrange("(p j) c -> p j c", j=PACK))
-            return raw
-
         def load_gain(name, src):
             tile = keep.tile([P, PACK], F32, name=name)
             nc.sync.dma_start(tile[:], src.rearrange("(p t) o -> p (t o)", t=PACK))
@@ -64,7 +59,6 @@ def tile_picked_kqorderwindwsum_none_p_kernel(
         gb_t = load_gain("gb_t", gb)
         n4_l = load_list("n4_l", n4)
         n3_l = load_list("n3_l", n3)
-        w1_raw = load_weight("w1_raw", w1)
         ga_t = load_gain("ga_t", ga)
         n1_l = load_list("n1_l", n1)
         n2_l = load_list("n2_l", n2)
@@ -83,7 +77,7 @@ def tile_picked_kqorderwindwsum_none_p_kernel(
         nc.vector.tensor_copy(xa[1][:], table_scales[:].indirect(offs_l[:]))
 
         def weave_weight(name, raws):
-            woven = keep.tile([P, PACK * N], BF16, name=name, align_bytes=64)
+            woven = keep.tile([P, PACK * N], BF16, name=name, tag=name, align_bytes=64)
             dst = woven[:].rearrange("p (t m j) -> p m j t", t=PACK, j=PACK)
             share = P // len(raws)
             for h, raw in enumerate(raws):
@@ -108,6 +102,8 @@ def tile_picked_kqorderwindwsum_none_p_kernel(
         w2_woven = weave_weight("w2_woven", w2_raw)
         w2q = mx_tiles("w2q")
         quantise(w2q, slice(0, N), w2_woven[:])
+        w1_raw = keep.tile([P, PACK, N], F32, name="w1_raw", tag="w2_woven", align_bytes=64)
+        nc.sync.dma_start(w1_raw[:], w1.rearrange("(p j) c -> p j c", j=PACK))
         nc.vector.tensor_copy(xb[0][:], table_words[:].indirect(two_l[:]))
         nc.vector.tensor_copy(xa[0][:], table_words[:].indirect(offs_l[:]))
 
@@ -120,22 +116,18 @@ def tile_picked_kqorderwindwsum_none_p_kernel(
         w1_woven = weave_weight("w1_woven", [w1_raw])
         w1q = mx_tiles("w1q")
 
-        z2_planes = keep.tile([P, PACK, N], BF16, name="z2_planes")
-        b4 = [keep.tile([P, N], F32, name="b4_%d" % t) for t in range(PACK)]
+        b4 = [keep.tile([P, N], F32, name="b4_%d" % t)[:] for t in range(2)]
         diff = [keep.tile([P, N], F32, name="diff%d" % t) for t in range(PACK)]
-        for step in range(PACK + 2):
+        for step in range(PACK + 1):
+            if step == 2:
+                quantise(w1q, slice(0, N), w1_woven[:])
+                late = keep.tile([P, 2, N], F32, name="b4_late", tag="w1_woven", align_bytes=64)
+                b4.extend([late[:, 0, :], late[:, 1, :]])
             if step < PACK:
-                nc.vector.tensor_copy(b4[step][:], wide[step][:].indirect(n4_l[:]))
+                nc.vector.tensor_copy(b4[step], wide[step][:].indirect(n4_l[:]))
             if 1 <= step <= PACK:
                 t = step - 1
-                nc.vector.tensor_tensor(diff[t][:], wide[t][:].indirect(n3_l[:]), b4[t][:], ALU.subtract)
-            if step >= 2:
-                t = step - 2
-                nc.vector.scalar_tensor_tensor(
-                    z2_planes[:, t, :], diff[t][:], gb_t[:, t : t + 1], b_banks[t][:], ALU.mult, ALU.mult
-                )
-            if step == 3:
-                quantise(w1q, slice(0, N), w1_woven[:])
+                nc.vector.tensor_tensor(diff[t][:], wide[t][:].indirect(n3_l[:]), b4[t], ALU.subtract)
 
         a_rows = [keep.tile([P, N], F32, name="a%d" % t) for t in range(PACK)]
         for t in range(PACK):
@@ -144,15 +136,15 @@ def tile_picked_kqorderwindwsum_none_p_kernel(
             nc.scalar.copy(a_rows[t][:], bank[:])
 
         z2_woven = keep.tile([P, PACK * N], BF16, name="z2_woven", align_bytes=64)
-        nc.scalar.copy(
-            z2_woven[:].rearrange("p (c i t) -> p c t i", i=4, t=PACK),
-            z2_planes[:].rearrange("p t (c i) -> p c t i", i=4),
-        )
-        z2q = mx_tiles("z2q")
+        z2_slots = z2_woven[:].rearrange("p (v t) -> p t v", t=PACK)
+        prod = keep.tile([P, PACK, N], F32, name="prod", tag="w1_woven", align_bytes=64)
+        for t in range(PACK):
+            nc.gpsimd.tensor_tensor(prod[:, t, :], diff[t][:], wide[t][:, :N], ALU.mult)
+            nc.scalar.activation(z2_slots[:, t], prod[:, t, :], ACT.Copy, scale=gb_t[:, t : t + 1])
 
         pa = keep.tile([P, PACK, W], F32, name="pa")
         pb = keep.tile([P, PACK, W], F32, name="pb")
-        ra = keep.tile([P, PACK, W], F32, name="ra")
+        ra = keep.tile([P, PACK, W], F32, name="ra", tag="ra", align_bytes=64)
         rb = keep.tile([P, PACK, W], F32, name="rb")
         for t in range(PACK):
             nc.vector.tensor_copy(pa[:, t, :], a_rows[t][:].indirect(n1_l[:]))
@@ -161,7 +153,6 @@ def tile_picked_kqorderwindwsum_none_p_kernel(
             pair = slice(2 * h, 2 * h + 2)
             nc.vector.tensor_tensor(ra[:, pair, :], pa[:, pair, :], pb[:, pair, :], ALU.max)
             nc.vector.tensor_tensor(rb[:, pair, :], pa[:, pair, :], pb[:, pair, :], ALU.min)
-        quantise(z2q, slice(0, N), z2_woven[:])
 
         dt_rows = [keep.tile([P, N], F32, name="dt%d" % t) for t in range(PACK)]
         z_woven = keep.tile([P, PACK * N], BF16, name="z_woven", align_bytes=64)
@@ -179,6 +170,11 @@ def tile_picked_kqorderwindwsum_none_p_kernel(
                         scale=ga_t[:, t : t + 1],
                     )
 
+        z2q = (
+            keep.tile([P, N], U32, name="z2q_codes", tag="ra", align_bytes=64),
+            keep.tile([P, N], U8, name="z2q_scales", align_bytes=64),
+        )
+        quantise(z2q, slice(0, N), z2_woven[:])
         zq = mx_tiles("zq")
         last = PACK - 1
         for u in range(PACK):
@@ -191,7 +187,7 @@ def tile_picked_kqorderwindwsum_none_p_kernel(
             quantise(zq, slice(P * u, P * (u + 1)), z_woven[:, N * u : N * (u + 1)])
 
         out_rows = out.rearrange("(p u) v -> u p v", u=PACK)
-        sig = [keep.tile([P, N], F32, name="sig%d" % u) for u in range(PACK)]
+        sig = [keep.tile([P, N], F32, name="sig%d" % u) for u in range(PACK + 1)]
         sig7 = [keep.tile([P, N], F32, name="sig7_%d" % u) for u in range(PACK)]
         for u in range(PACK):
             if u == 0:
@@ -206,23 +202,27 @@ def tile_picked_kqorderwindwsum_none_p_kernel(
                 bank = psum.tile([P, N], F32, name="bank%d" % u)
                 product(bank[:], zq, u, z2q, slice(0, N))
                 nc.scalar.activation(wide[u][:, :N], bank[:], ACT.Copy, scale=0.0625)
-                nc.scalar.activation(sig[u][:], bank[:], ACT.Sigmoid, scale=0.0625)
+                if u < PACK - 1:
+                    nc.scalar.activation(sig[u][:], bank[:], ACT.Sigmoid, scale=0.0625)
+                else:
+                    for h in range(2):
+                        nc.scalar.activation(sig[u + h][:, : N // 2], bank[:, halves[h]], ACT.Sigmoid, scale=0.0625)
             nc.scalar.activation(sig7[u][:], wide[u][:].indirect(n7_l[:]), ACT.Sigmoid)
 
         pieces = [(u, 0, N) for u in range(PACK - 1)] + [(PACK - 1, 0, N // 2), (PACK - 1, N // 2, N)]
         term5 = [keep.tile([P, N], F32, name="term5_%d" % u) for u in range(PACK)]
         term6 = [keep.tile([P, N], F32, name="term6_%d" % u) for u in range(PACK)]
-        total = [keep.tile([P, N], F32, name="total%d" % u) for u in range(PACK)]
 
-        def finish(piece):
+        def finish(piece, total):
             u, c0, c1 = piece
-            nc.vector.tensor_tensor(total[u][:, c0:c1], term5[u][:, c0:c1], term6[u][:, c0:c1], ALU.add)
-            nc.sync.dma_start(out_rows[u][:, c0:c1], total[u][:, c0:c1])
+            nc.vector.tensor_tensor(total, term5[u][:, c0:c1], term6[u][:, c0:c1], ALU.add)
+            nc.sync.dma_start(out_rows[u][:, c0:c1], total)
 
         for i, (u, c0, c1) in enumerate(pieces):
             entries = slice(c0 // 16, c1 // 16)
-            nc.vector.tensor_tensor(term5[u][:, c0:c1], wide[u][:].indirect(n5_l[:, entries]), sig[u][:, c0:c1], ALU.mult)
-            if i >= 1:
-                finish(pieces[i - 1])
+            nc.vector.tensor_tensor(term5[u][:, c0:c1], wide[u][:].indirect(n5_l[:, entries]), sig[i][:, : c1 - c0], ALU.mult)
             nc.vector.tensor_tensor(term6[u][:, c0:c1], wide[u][:].indirect(n6_l[:, entries]), sig7[u][:, c0:c1], ALU.mult)
-        finish(pieces[-1])
+            if i >= 1:
+                before = pieces[i - 1]
+                finish(before, sig[i][:, : before[2] - before[1]])
+        finish(pieces[-1], sig[0][:, : N // 2])

from contextlib import ExitStack

import concourse.mybir as mybir

F32 = mybir.dt.float32
BF16 = mybir.dt.bfloat16
U32 = mybir.dt.uint32
I32 = mybir.dt.int32
U16 = mybir.dt.uint16
U8 = mybir.dt.uint8
FP8X4 = mybir.dt.float8_e4m3fn_x4
ALU = mybir.AluOpType
ACT = mybir.ActivationFunctionType

P = 128
PACK = 4
T = 2048
N = 512
W = 256
FLOPS = 3 * 2 * 512 * 512 * 512


def tile_picked_kqorderwindwsum_none_p_kernel(
    tc, x_words, x_scales, w1, w2, ga, gb, offs, two, n1, n2, n3, n4, n5, n6, n7, out
):
    nc = tc.nc
    with ExitStack() as ctx:
        keep = ctx.enter_context(tc.tile_pool(name="keep", bufs=1))
        psum = ctx.enter_context(tc.psum_pool(name="psum", bufs=1))

        def load_list(name, src):
            tile = keep.tile([P, src.shape[1]], U16, name=name)
            nc.sync.dma_start(tile[:], src)
            return tile

        def load_gain(name, src):
            tile = keep.tile([P, PACK], F32, name=name)
            nc.sync.dma_start(tile[:], src.rearrange("(p t) o -> p (t o)", t=PACK))
            return tile

        table_scales = keep.tile([P, T], U8, name="table_scales", align_bytes=64)
        nc.vector.memset(table_scales[:].bitcast(I32), 0)
        warm = keep.tile([P, 2], F32, name="warm")
        nc.vector.memset(warm[:, 0:1], 0.0)

        two_l = load_list("two_l", two)
        offs_l = load_list("offs_l", offs)
        w2_view = w2.rearrange("(p j) c -> p j c", j=PACK)
        w2_raw = [keep.tile([P, PACK, N // 2], F32, name="w2_raw%d" % h) for h in range(2)]
        nc.sync.dma_start(w2_raw[0][:], w2_view[:, :, : N // 2])
        for q in range(4):
            nc.sync.dma_start(
                table_scales[32 * q : 32 * q + 4, :].bitcast(I32), x_scales[0, 4 * q : 4 * q + 4, :].bitcast(I32)
            )
        nc.sync.dma_start(w2_raw[1][:], w2_view[:, :, N // 2 :])
        table_words = keep.tile([P, T], U32, name="table_words", align_bytes=64)
        nc.sync.dma_start(table_words[:].bitcast(I32), x_words[0].rearrange("p n t -> p (n t)").bitcast(I32))
        nc.scalar.activation(warm[:, 1:2], warm[:, 0:1], ACT.Sigmoid)
        gb_t = load_gain("gb_t", gb)
        n4_l = load_list("n4_l", n4)
        n3_l = load_list("n3_l", n3)
        ga_t = load_gain("ga_t", ga)
        n1_l = load_list("n1_l", n1)
        n2_l = load_list("n2_l", n2)
        n5_l = load_list("n5_l", n5)
        n6_l = load_list("n6_l", n6)
        n7_l = load_list("n7_l", n7)

        def mx_tiles(name):
            codes = keep.tile([P, N], U32, name=name + "_codes", align_bytes=64)
            scales = keep.tile([P, N], U8, name=name + "_scales", align_bytes=64)
            return codes, scales

        xb = mx_tiles("xb")
        xa = mx_tiles("xa")
        nc.vector.tensor_copy(xb[1][:], table_scales[:].indirect(two_l[:]))
        nc.vector.tensor_copy(xa[1][:], table_scales[:].indirect(offs_l[:]))

        def weave_weight(name, raws):
            woven = keep.tile([P, PACK * N], BF16, name=name, tag=name, align_bytes=64)
            dst = woven[:].rearrange("p (t m j) -> p m j t", t=PACK, j=PACK)
            share = P // len(raws)
            for h, raw in enumerate(raws):
                nc.scalar.copy(dst[:, h * share : (h + 1) * share], raw[:].rearrange("p j (m t) -> p m j t", t=PACK))
            return woven

        def quantise(pair, cols, src):
            nc.vector.quantize_mx(out=pair[0][:, cols].bitcast(FP8X4), scales=pair[1][:, cols], in_=src)

        def product(acc, stationary, t, moving, span):
            cols = slice(P * t, P * (t + 1))
            nc.tensor.matmul_mx(
                out=acc,
                lhsT=stationary[0][:, cols].bitcast(FP8X4),
                lhsT_scale=stationary[1][:, cols],
                rhs=moving[0][:, span].bitcast(FP8X4),
                rhs_scale=moving[1][:, span],
                start=True,
                stop=True,
            )

        w2_woven = weave_weight("w2_woven", w2_raw)
        w2q = mx_tiles("w2q")
        quantise(w2q, slice(0, N), w2_woven[:])
        w1_raw = keep.tile([P, PACK, N], F32, name="w1_raw", tag="w2_woven", align_bytes=64)
        nc.sync.dma_start(w1_raw[:], w1.rearrange("(p j) c -> p j c", j=PACK))
        nc.vector.tensor_copy(xb[0][:], table_words[:].indirect(two_l[:]))
        nc.vector.tensor_copy(xa[0][:], table_words[:].indirect(offs_l[:]))

        wide = [keep.tile([P, 2 * N], F32, name="wide%d" % t) for t in range(PACK)]
        b_banks = [psum.tile([P, N], F32, name="bank%d" % t) for t in range(PACK)]
        for t in range(PACK):
            product(b_banks[t][:], w2q, t, xb, slice(0, N))
            nc.scalar.copy(wide[t][:, :N], b_banks[t][:])

        w1_woven = weave_weight("w1_woven", [w1_raw])
        w1q = mx_tiles("w1q")

        b4 = [keep.tile([P, N], F32, name="b4_%d" % t)[:] for t in range(2)]
        diff = [keep.tile([P, N], F32, name="diff%d" % t) for t in range(PACK)]
        for step in range(PACK + 1):
            if step == 2:
                quantise(w1q, slice(0, N), w1_woven[:])
                late = keep.tile([P, 2, N], F32, name="b4_late", tag="w1_woven", align_bytes=64)
                b4.extend([late[:, 0, :], late[:, 1, :]])
            if step < PACK:
                nc.vector.tensor_copy(b4[step], wide[step][:].indirect(n4_l[:]))
            if 1 <= step <= PACK:
                t = step - 1
                nc.vector.tensor_tensor(diff[t][:], wide[t][:].indirect(n3_l[:]), b4[t], ALU.subtract)

        a_rows = [keep.tile([P, N], F32, name="a%d" % t) for t in range(PACK)]
        for t in range(PACK):
            bank = psum.tile([P, N], F32, name="bank%d" % (PACK + t))
            product(bank[:], w1q, t, xa, slice(0, N))
            nc.scalar.copy(a_rows[t][:], bank[:])

        z2_woven = keep.tile([P, PACK * N], BF16, name="z2_woven", align_bytes=64)
        z2_slots = z2_woven[:].rearrange("p (v t) -> p t v", t=PACK)
        prod = keep.tile([P, PACK, N], F32, name="prod", tag="w1_woven", align_bytes=64)
        for t in range(PACK):
            nc.gpsimd.tensor_tensor(prod[:, t, :], diff[t][:], wide[t][:, :N], ALU.mult)
            nc.scalar.activation(z2_slots[:, t], prod[:, t, :], ACT.Copy, scale=gb_t[:, t : t + 1])

        pa = keep.tile([P, PACK, W], F32, name="pa")
        pb = keep.tile([P, PACK, W], F32, name="pb")
        ra = keep.tile([P, PACK, W], F32, name="ra", tag="ra", align_bytes=64)
        rb = keep.tile([P, PACK, W], F32, name="rb")
        for t in range(PACK):
            nc.vector.tensor_copy(pa[:, t, :], a_rows[t][:].indirect(n1_l[:]))
            nc.vector.tensor_copy(pb[:, t, :], a_rows[t][:].indirect(n2_l[:]))
        for h in range(2):
            pair = slice(2 * h, 2 * h + 2)
            nc.vector.tensor_tensor(ra[:, pair, :], pa[:, pair, :], pb[:, pair, :], ALU.max)
            nc.vector.tensor_tensor(rb[:, pair, :], pa[:, pair, :], pb[:, pair, :], ALU.min)

        dt_rows = [keep.tile([P, N], F32, name="dt%d" % t) for t in range(PACK)]
        z_woven = keep.tile([P, PACK * N], BF16, name="z_woven", align_bytes=64)
        z_slots = z_woven[:].rearrange("p (u m t) -> p t u m", u=PACK, t=PACK)
        for h in range(2):
            for t in (2 * h, 2 * h + 1):
                nc.vector.tensor_copy(dt_rows[t][:].indirect(n1_l[:]), ra[:, t, :])
            for t in (2 * h, 2 * h + 1):
                nc.vector.tensor_copy(dt_rows[t][:].indirect(n2_l[:]), rb[:, t, :])
                if t < PACK - 1:
                    nc.scalar.activation(
                        z_slots[:, t],
                        dt_rows[t][:].rearrange("p (m u) -> p u m", u=PACK),
                        ACT.Copy,
                        scale=ga_t[:, t : t + 1],
                    )

        z2q = (
            keep.tile([P, N], U32, name="z2q_codes", tag="ra", align_bytes=64),
            keep.tile([P, N], U8, name="z2q_scales", align_bytes=64),
        )
        quantise(z2q, slice(0, N), z2_woven[:])
        zq = mx_tiles("zq")
        last = PACK - 1
        for u in range(PACK):
            nc.scalar.activation(
                z_slots[:, last, u],
                dt_rows[last][:].rearrange("p (m u) -> p u m", u=PACK)[:, u],
                ACT.Copy,
                scale=ga_t[:, last : last + 1],
            )
            quantise(zq, slice(P * u, P * (u + 1)), z_woven[:, N * u : N * (u + 1)])

        out_rows = out.rearrange("(p u) v -> u p v", u=PACK)
        sig = [keep.tile([P, N], F32, name="sig%d" % u) for u in range(PACK + 1)]
        sig7 = [keep.tile([P, N], F32, name="sig7_%d" % u) for u in range(PACK)]
        for u in range(PACK):
            if u == 0:
                halves = [slice(0, N // 2), slice(N // 2, N)]
                banks = [psum.tile([P, N], F32, name="bank%d" % (PACK * h)) for h in range(2)]
                for h in range(2):
                    product(banks[h][:, : N // 2], zq, u, z2q, halves[h])
                for h in range(2):
                    nc.scalar.activation(sig[u][:, halves[h]], banks[h][:, : N // 2], ACT.Sigmoid, scale=0.0625)
                    nc.vector.tensor_scalar_mul(wide[u][:, halves[1 - h]], banks[1 - h][:, : N // 2], 0.0625)
            else:
                bank = psum.tile([P, N], F32, name="bank%d" % u)
                product(bank[:], zq, u, z2q, slice(0, N))
                nc.scalar.activation(wide[u][:, :N], bank[:], ACT.Copy, scale=0.0625)
                if u < PACK - 1:
                    nc.scalar.activation(sig[u][:], bank[:], ACT.Sigmoid, scale=0.0625)
                else:
                    for h in range(2):
                        nc.scalar.activation(sig[u + h][:, : N // 2], bank[:, halves[h]], ACT.Sigmoid, scale=0.0625)
            nc.scalar.activation(sig7[u][:], wide[u][:].indirect(n7_l[:]), ACT.Sigmoid)

        pieces = [(u, 0, N) for u in range(PACK - 1)] + [(PACK - 1, 0, N // 2), (PACK - 1, N // 2, N)]
        term5 = [keep.tile([P, N], F32, name="term5_%d" % u) for u in range(PACK)]
        term6 = [keep.tile([P, N], F32, name="term6_%d" % u) for u in range(PACK)]

        def finish(piece, total):
            u, c0, c1 = piece
            nc.vector.tensor_tensor(total, term5[u][:, c0:c1], term6[u][:, c0:c1], ALU.add)
            nc.sync.dma_start(out_rows[u][:, c0:c1], total)

        for i, (u, c0, c1) in enumerate(pieces):
            entries = slice(c0 // 16, c1 // 16)
            nc.vector.tensor_tensor(term5[u][:, c0:c1], wide[u][:].indirect(n5_l[:, entries]), sig[i][:, : c1 - c0], ALU.mult)
            nc.vector.tensor_tensor(term6[u][:, c0:c1], wide[u][:].indirect(n6_l[:, entries]), sig7[u][:, c0:c1], ALU.mult)
            if i >= 1:
                before = pieces[i - 1]
                finish(before, sig[i][:, : before[2] - before[1]])
        finish(pieces[-1], sig[0][:, : N // 2])
